import numpy as np
import ml_dtypes


def mxq(x, axis, fmt="e4m3"):
    dtype, down = {"e4m3": (ml_dtypes.float8_e4m3fn, 7), "e5m2": (ml_dtypes.float8_e5m2, 14)}[fmt]
    v = np.moveaxis(np.asarray(x, np.float32).astype(ml_dtypes.bfloat16).astype(np.float64), axis, -1)
    blocks = v.reshape(v.shape[:-1] + (-1, 32))
    amax = np.abs(blocks).max(-1, keepdims=True)
    byte = np.maximum(np.where(amax > 0, np.frexp(amax)[1] - 1 + 127, 0) - down, 1)
    scale = np.exp2(byte - 127.0)
    codes = (blocks / scale).astype(np.float32).astype(dtype).astype(np.float64)
    return np.moveaxis((codes * scale).reshape(v.shape), -1, axis)


WIDE = False


def mx_kscale(k):
    if not WIDE:
        return np.ones(k)
    levels = np.array([10, -10, 5, -5, 0])
    if k % 512:
        return np.exp2(np.random.permutation(np.resize(levels, k // 32))).repeat(32)
    a = np.empty((k // 512, 16))
    for p in range(k // 512):
        a[p, :8] = np.random.permutation(np.resize(levels, 8))
        for g in range(8):
            far = levels[np.abs(levels - a[p, g]) >= 10]
            a[p, g + 8] = far[np.random.randint(len(far))]
    return np.exp2(a.ravel()).repeat(32)


def f64(x):
    return np.asarray(x).astype(np.float64)


def striped(idx):
    return np.tile(idx.reshape(-1, 16).T, (8, 1)).astype(np.uint16)


def unstriped(offs):
    return offs[:16].T.reshape(-1).astype(np.int64)


E2M1 = np.array([0.0, 0.5, 1.0, 1.5, 2.0, 3.0, 4.0, 6.0, -0.0, -0.5, -1.0, -1.5, -2.0, -3.0, -4.0, -6.0])


def pack_weight(w, fmt):
    k, n = w.shape
    w = f64(np.asarray(w, np.float32).astype(ml_dtypes.bfloat16)).reshape(k // 32, 32, n)
    amax = np.abs(w).max(1)
    if fmt == "e4m3":
        byte = np.frexp(amax)[1] - 1 + 127 - 7
    else:
        mant, ex = np.frexp(amax / 6.0)
        byte = np.where(mant > 0.5, ex, ex - 1) + 127
    byte = np.clip(np.where(amax > 0, byte, 1), 1, 254)
    scaled = (w * np.exp2(127.0 - byte)[:, None, :]).reshape(k, n).astype(np.float32)
    by_word = np.ascontiguousarray(scaled.reshape(k // 512, 128, 4, n).transpose(0, 1, 3, 2))
    if fmt == "e4m3":
        words = by_word.astype(ml_dtypes.float8_e4m3fn).view(np.uint8)
    else:
        c = by_word.astype(ml_dtypes.float4_e2m1fn).view(np.uint8) & 0xF
        words = (c[..., 0::2] | (c[..., 1::2] << 4)).reshape(k // 512, 128, 2 * n)
    return np.ascontiguousarray(words), np.ascontiguousarray(byte.astype(np.uint8).reshape(k // 512, 16, n))


def unpack_weight(words, scales, fmt):
    g, _, n = scales.shape
    words = np.ascontiguousarray(words).reshape(g, 128, n, -1)
    if fmt == "e4m3":
        vals = words.view(ml_dtypes.float8_e4m3fn).astype(np.float64)
    else:
        nib = np.empty((g, 128, n, 4), np.uint8)
        nib[..., 0::2] = words & 0xF
        nib[..., 1::2] = words >> 4
        vals = E2M1[nib]
    vals = vals * np.repeat(np.exp2(scales.astype(np.float64) - 127.0), 8, axis=1)[..., None]
    return vals.transpose(0, 1, 3, 2).reshape(g * 512, n)


def gelu(v):
    return 0.5 * v * (1.0 + np.tanh(np.sqrt(2.0 / np.pi) * (v + 0.044715 * v**3)))


K, T, S, H, N, T2, P = 1024, 4096, 1024, 1024, 384, 2048, 1024


def setup_inputs():
    n = np.random.standard_normal
    s = mx_kscale(K)[:, None]
    u = mx_kscale(H)[:, None]
    d = {}
    d["tab_words"], d["tab_scales"] = pack_weight(n((K, T)) * s, "e4m3")
    d["offs"] = striped(np.random.permutation(T)[:S])
    d["w1"] = (1.4 * n((K, H)) / K**0.5 / s).astype(np.float32)
    d["base"] = (1.2 * n((H, S))).astype(np.float32)
    d["w2_words"], d["w2_scales"] = pack_weight(0.6 * n((K, H)) / K**0.5 / s, "e2m1")
    d["wgs"] = np.exp(0.3 * n((128, S))).astype(np.float32)
    d["page0"] = n((H, T2)).astype(np.float32)
    d["offs2"] = striped(np.random.permutation(T2)[:S])
    d["offs3"] = striped(np.random.permutation(T2)[:P])
    d["gain"] = (np.exp(0.3 * n(H)) * u[:, 0]).astype(np.float32)
    d["w3"] = (1.2 * n((H, N)) / H**0.5 / u).astype(np.float32)
    d["w4"] = (-0.8 * n((K, N)) / K**0.5 / s).astype(np.float32)
    d["wgo"] = np.exp(0.3 * n((128, P))).astype(np.float32)
    d["page1"] = n((N, T2)).astype(np.float32)
    d["offs4"] = striped(np.random.permutation(T2)[:P])
    return d


def reference(tab_words, tab_scales, offs, w1, base, w2_words, w2_scales, wgs, page0, offs2, offs3,
              gain, w3, w4, wgo, page1, offs4):
    v = unpack_weight(tab_words, tab_scales, "e4m3")[:, unstriped(offs)]
    a = mxq(f64(w1), 0, "e4m3").T @ v
    b = unpack_weight(w2_words, w2_scales, "e2m1").T @ v
    h = np.tanh(a + f64(base)) + b
    page = f64(page0).copy()
    page[:, unstriped(offs2)] = np.tile(f64(wgs), (H // 128, 1)) * h
    x = mxq(page[:, unstriped(offs3)] * f64(gain)[:, None], 0, "e4m3")
    e = mxq(f64(w3), 0, "e4m3").T @ x + mxq(f64(w4), 0, "e4m3").T @ v
    y = np.log(np.square(e) + 1.0)
    out = f64(page1).copy()
    out[:, unstriped(offs4)] = np.tile(f64(wgo), (N // 128, 1)) * y
    return out

@@ -1,0 +1,412 @@
+from contextlib import ExitStack
+
+import concourse.mybir as mybir
+from concourse.masks import make_identity
+
+K, T, S, H, N, T2 = 1024, 4096, 1024, 1024, 384, 2048
+FLOPS = 2 * S * (2 * K * H + H * N + K * N)
+
+F32 = mybir.dt.float32
+BF16 = mybir.dt.bfloat16
+I32 = mybir.dt.int32
+U32 = mybir.dt.uint32
+U16 = mybir.dt.uint16
+U8 = mybir.dt.uint8
+FP8X4 = mybir.dt.float8_e4m3fn_x4
+FP4X4 = mybir.dt.float4_e2m1fn_x4
+ACT = mybir.ActivationFunctionType
+MULT = mybir.AluOpType.mult
+ADD = mybir.AluOpType.add
+
+P = 128
+HALF = 512
+LIST_HALF = HALF // 16
+QUADS = (0, 2, 1, 3)
+
+
+def tile_list_radon_mitigation_page_kernel(
+    tc, tab_words, tab_scales, offs, w1, base, w2_words, w2_scales, wgs, page0, offs2, offs3,
+    gain, w3, w4, wgo, page1, offs4, out,
+):
+    nc = tc.nc
+    with ExitStack() as ctx:
+        sb = ctx.enter_context(tc.tile_pool(name="sb", bufs=1))
+        ps = ctx.enter_context(tc.psum_pool(name="ps", bufs=1))
+
+        def tile(shape, dtype, name, tag=None):
+            return sb.tile(shape, dtype, name=name, tag=tag or name, align_bytes=64)
+
+        def bank(name, tag):
+            return ps.tile([P, HALF], F32, name=name, tag=tag)
+
+        def half(u):
+            return slice(u * HALF, (u + 1) * HALF)
+
+        def list_half(lst, u):
+            return lst[:, u * LIST_HALF : (u + 1) * LIST_HALF]
+
+        def load_list(src, name):
+            lst = tile([P, S // 16], U16, name)
+            nc.sync.dma_start(lst[:], src)
+            return lst
+
+        def load_rows(src, b, t, name, tag):
+            dst = tile([P, src.shape[1]], F32, name, tag)
+            nc.sync.dma_start(dst[:], src[half(b), :].rearrange("(p t) j -> p t j", t=4)[:, t, :])
+            return dst
+
+        def load_weight(src, a, cols, name, tag):
+            raw = tile([P, 4, cols.stop - cols.start], F32, name, tag)
+            nc.sync.dma_start(raw[:], src[half(a), cols].rearrange("(p i) c -> p i c", i=4))
+            return raw
+
+        def load_w2(b):
+            words = tile([P, 2, 2 * HALF], U8, "w2w%d" % b)
+            nc.sync.dma_start(
+                words[:].bitcast(I32),
+                w2_words[:, :, 2 * HALF * b : 2 * HALF * (b + 1)].rearrange("a p c -> p a c").bitcast(I32),
+            )
+            return words
+
+        def load_wgs(t0, t1, name, pieces):
+            dst = tile([P, t1 - t0, S], F32, name)
+            rows = wgs.rearrange("(q t) j -> q t j", t=4)[:, t0:t1, :]
+            for cols in pieces:
+                for quad in QUADS:
+                    nc.sync.dma_start(dst[32 * quad : 32 * quad + 32, :, cols], rows[:, :, cols])
+            return dst
+
+        tab_planes = tile([P, 2, T], U8, "tab_planes")
+        w2_planes = tile([P, 2, H], U8, "w2_planes")
+        nc.vector.memset(tab_planes[:, 0, :].bitcast(I32), 0)
+        nc.gpsimd.memset(tab_planes[:, 1, :].bitcast(I32), 0)
+        nc.vector.memset(w2_planes[:].bitcast(I32), 0)
+        ident = tile([P, P], F32, "ident")
+        make_identity(nc, ident[:])
+
+        idx = load_list(offs, "idx")
+        tab = [tile([P, T], I32, "tab%d" % a, "big%d" % a) for a in range(2)]
+
+        def load_tab(a):
+            nc.sync.dma_start(tab[a][:], tab_words[a].rearrange("p t i -> p (t i)").bitcast(I32))
+
+        def load_planes(planes, src):
+            for quad in QUADS:
+                nc.sync.dma_start(
+                    planes[32 * quad : 32 * quad + 4].bitcast(I32),
+                    src[:, 4 * quad : 4 * quad + 4, :].rearrange("a r c -> r a c").bitcast(I32),
+                )
+
+        load_tab(0)
+        w2w = {0: load_w2(0)}
+        idx2 = load_list(offs2, "idx2")
+        idx3 = load_list(offs3, "idx3")
+        load_planes(tab_planes, tab_scales)
+        w1_raw = {(0, 0): load_weight(w1, 0, half(0), "w1raw00", "raw0")}
+        load_tab(1)
+        load_planes(w2_planes, w2_scales)
+        w1_raw[0, 1] = load_weight(w1, 1, half(0), "w1raw01", "raw1")
+        base_t = {0: load_rows(base, 0, 0, "base0", "base0")}
+        page = {0: load_rows(page0, 0, 0, "page0", "page0")}
+        wgs0 = load_wgs(0, 1, "wgs0", (half(0), half(1)))
+        base_t[1] = load_rows(base, 0, 1, "base1", "base1")
+        page[1] = load_rows(page0, 0, 1, "page1", "page1")
+        wgs1 = load_wgs(1, 2, "wgs1", (slice(0, S),))
+        base_t[2] = load_rows(base, 0, 2, "base2", "base2")
+        page[2] = load_rows(page0, 0, 2, "page2", "page2")
+        wgs23 = load_wgs(2, 4, "wgs23", (slice(0, S),))
+        for a in range(2):
+            w1_raw[1, a] = load_weight(w1, a, half(1), "w1raw1%d" % a, "raw%d" % (2 + a))
+        w2w[1] = load_w2(1)
+        page[3] = load_rows(page0, 0, 3, "page3", "page3")
+        gains = tile([P, 2, 4], F32, "gains")
+        nc.sync.dma_start(gains[:], gain.rearrange("(b p t) -> p b t", b=2, t=4))
+        idx4 = load_list(offs4, "idx4")
+
+        v_planes = [tile([P, S], U8, "v_plane%d" % a) for a in range(2)]
+        for a in range(2):
+            nc.vector.tensor_copy(v_planes[a][:], tab_planes[:, a, :].indirect(idx[:]))
+
+        w1_codes, w1_planes = {}, {}
+
+        def quantize_w1(b, a, t0, t1, copy, tag, pieces=1):
+            grouped = tile([P, t1 - t0, P, 4], BF16, "w1g%d%d%d" % (b, a, t0), tag)
+            step = P // pieces
+            for m0 in range(0, P, step):
+                copy(
+                    grouped[:].rearrange("p t m i -> p m i t")[:, m0 : m0 + step],
+                    w1_raw[b, a][:].rearrange("p i (m t) -> p m i t", t=4)[:, m0 : m0 + step, :, t0:t1],
+                )
+            flat = grouped[:].rearrange("p t m i -> p (t m i)")
+            done = 0
+            for width in (4, 2, 1):
+                if (t1 - t0) & width:
+                    cols = slice((t0 + done) * P, (t0 + done + width) * P)
+                    nc.vector.quantize_mx(
+                        out=w1_codes[b][:, a, cols].bitcast(FP8X4),
+                        scales=w1_planes[b][:, a, cols],
+                        in_=flat[:, done * HALF : (done + width) * HALF],
+                    )
+                    done += width
+
+        for b in range(2):
+            w1_codes[b] = tile([P, 2, HALF], U32, "w1c%d" % b, "codes%d" % b)
+            w1_planes[b] = tile([P, 2, HALF], U8, "w1s%d" % b)
+        v_words = [tile([P, S], U32, "v%d" % a) for a in range(2)]
+        nc.vector.tensor_copy(v_words[0][:], tab[0][:].bitcast(U32).indirect(idx[:]))
+        for u in range(2):
+            nc.vector.tensor_copy(v_words[1][:, half(u)], tab[1][:].bitcast(U32).indirect(list_half(idx, u)))
+
+        quantize_w1(0, 0, 0, 4, nc.scalar.copy, "grp0")
+        quantize_w1(0, 1, 0, 1, nc.vector.tensor_copy, "grp1")
+        b_t = {}
+
+        def skip_product(b, u):
+            b_t[b, u] = tile([P, 4, 4, P], F32, "bt%d%d" % (b, u))
+            for jb in range(4):
+                cols = slice(u * HALF + jb * P, u * HALF + (jb + 1) * P)
+                acc = bank("pb%d%d%d" % (b, u, jb), "pb%d" % jb)
+                for a in range(2):
+                    nc.tensor.matmul_mx(
+                        out=acc[:],
+                        lhsT=v_words[a][:, cols].bitcast(FP8X4),
+                        lhsT_scale=v_planes[a][:, cols],
+                        rhs=w2w[b][:, a, :].bitcast(FP4X4),
+                        rhs_scale=w2_planes[:, a, half(b)],
+                        start=(a == 0),
+                        stop=(a == 1),
+                    )
+                nc.scalar.copy(b_t[b, u][:, jb], acc[:].rearrange("p (q t) -> p t q", t=4))
+
+        def add_transposed(acc, *terms):
+            for n, blocks in enumerate(terms):
+                for jb in range(4):
+                    nc.tensor.matmul(
+                        acc[:, jb * P : (jb + 1) * P], lhsT=blocks(jb), rhs=ident[:], is_transpose=True,
+                        start=(n == 0 and jb == 0), stop=(n == len(terms) - 1 and jb == 3),
+                    )
+
+        h = {}
+        tanh_t = {}
+
+        def first_product(s, u):
+            b, t = divmod(s, 4)
+            rows = slice(t * P, (t + 1) * P)
+            acc = bank("pa%d%d" % (s, u), "state%d" % u)
+            for a in range(2):
+                nc.tensor.matmul_mx(
+                    out=acc[:],
+                    lhsT=w1_codes[b][:, a, rows].bitcast(FP8X4),
+                    lhsT_scale=w1_planes[b][:, a, rows],
+                    rhs=v_words[a][:, half(u)].bitcast(FP8X4),
+                    rhs_scale=v_planes[a][:, half(u)],
+                    start=(a == 0),
+                    stop=(a == 1),
+                )
+            return acc
+
+        def first_state():
+            th = []
+            for u in range(2):
+                acc = first_product(0, u)
+                pre = tile([P, HALF], F32, "pre_first%d" % u, "asb%d" % u)
+                nc.vector.tensor_tensor(pre[:], acc[:], base_t[0][:, half(u)], ADD)
+                th.append(tile([P, HALF], F32, "th_first%d" % u, "th%d" % u))
+                nc.scalar.activation(th[u][:], pre[:], ACT.Tanh)
+            quantize_w1(0, 1, 1, 4, nc.vector.tensor_copy, "grp1")
+            for u in range(2):
+                skip_product(0, u)
+                post = bank("post_first%d" % u, "t1%d" % u)
+                add_transposed(post, lambda jb: b_t[0, u][:, jb, 0, :])
+                nc.vector.tensor_tensor(h[0][:, half(u)], post[:], th[u][:], ADD)
+                nc.vector.tensor_tensor(
+                    page[0][:].indirect(list_half(idx2, u)), h[0][:, half(u)], wgs0[:, 0, half(u)], MULT
+                )
+
+        def state_half(s, u):
+            b, t = divmod(s, 4)
+            acc = first_product(s, u)
+            a_sb = tile([P, HALF], F32, "a%d%d" % (s, u), "asb%d" % u)
+            nc.scalar.copy(a_sb[:], acc[:])
+            pre = bank("pre%d%d" % (s, u), "t1%d" % u)
+            add_transposed(
+                pre,
+                lambda jb: base_t[s][:, u * HALF + jb * P : u * HALF + (jb + 1) * P],
+                lambda jb: a_sb[:, jb * P : (jb + 1) * P],
+            )
+            th = tile([P, HALF], F32, "th%d%d" % (s, u), "th%d" % u)
+            nc.scalar.activation(th[:], pre[:], ACT.Tanh)
+            tanh_t[s, u] = th
+            if s == 4:
+                skip_product(b, u)
+            post = bank("post%d%d" % (s, u), "state%d" % u)
+            add_transposed(post, lambda jb: th[:, jb * P : (jb + 1) * P], lambda jb: b_t[b, u][:, jb, t, :])
+            nc.scalar.copy(h[s][:, half(u)], post[:])
+
+        def wgs_of(s):
+            t = s % 4
+            return (wgs0[:, 0, :], wgs1[:, 0, :], wgs23[:, 0, :], wgs23[:, 1, :])[t]
+
+        picked = {}
+
+        def one_slice(s):
+            b, t = divmod(s, 4)
+            h[s] = tile([P, S], F32, "h%d" % s, "h%d" % (s % 3))
+            if s == 0:
+                first_state()
+            else:
+                for u in range(2):
+                    state_half(s, u)
+                nc.vector.tensor_tensor(page[s][:].indirect(idx2[:]), h[s][:], wgs_of(s), MULT)
+            if b == 0:
+                nc.vector.tensor_copy(picked[0][:, t, :], page[s][:].indirect(idx3[:]))
+            else:
+                nc.vector.tensor_copy(picked[1][:, t, :], page[s][:].indirect(list_half(idx3, 0)))
+
+        def later_loads(s):
+            b, t = divmod(s, 4)
+            base_t[s] = load_rows(base, b, t, "base%d" % s, "base%d" % (s % 3))
+            if s >= 4:
+                page[s] = load_rows(page0, b, t, "page%d" % s, "page%d" % (s % 4))
+
+        picked[0] = tile([P, 4, S], F32, "picked0", "big0")
+        picked[1] = tile([P, 4, HALF], F32, "picked1", "big1")
+        one_slice(0)
+        later_loads(3)
+        one_slice(1)
+        for a in range(2):
+            quantize_w1(1, a, 0, 4, nc.scalar.copy, "grp%d" % a, 4)
+        later_loads(4)
+
+        w34_codes = tile([P, 4, N], U32, "w34c")
+        w34_planes = tile([P, 4, N], U8, "w34s")
+        for m, src in enumerate((w4, w3)):
+            grouped = tile([P, 2, N, 4], BF16, "w34g%d" % m, "raw%d" % (2 + m))
+            for a in range(2):
+                raw = load_weight(src, a, slice(0, N), "w34raw%d%d" % (m, a), "raw%d" % a)
+                for c0 in range(0, N // 4, 32):
+                    nc.scalar.copy(
+                        grouped[:, a].rearrange("p (c e) i -> p c i e", e=4)[:, c0 : c0 + 32],
+                        raw[:].rearrange("p i (c e) -> p c i e", e=4)[:, c0 : c0 + 32],
+                    )
+            flat_in = grouped[:].rearrange("p a c i -> p (a c i)")
+            flat_codes = w34_codes[:, 2 * m : 2 * m + 2, :].rearrange("p a c -> p (a c)")
+            flat_planes = w34_planes[:, 2 * m : 2 * m + 2, :].rearrange("p a c -> p (a c)")
+            for c0, c1 in ((0, 512), (512, 768)):
+                nc.vector.quantize_mx(
+                    out=flat_codes[:, c0:c1].bitcast(FP8X4),
+                    scales=flat_planes[:, c0:c1],
+                    in_=flat_in[:, 4 * c0 : 4 * c1],
+                )
+
+        x_codes, x_planes = {}, {}
+
+        def scale_rows(dst, src, s):
+            b, t = divmod(s, 4)
+            nc.scalar.activation(dst[:, t, :], src, ACT.Copy, scale=gains[:, b, t : t + 1])
+
+        def interleave(scaled, b, u, tag, pieces=1):
+            grouped = tile([P, HALF, 4], BF16, "xg%d%d" % (b, u), tag)
+            step = HALF // 4 // pieces
+            for c0 in range(0, HALF // 4, step):
+                nc.scalar.copy(
+                    grouped[:].rearrange("p (c e) t -> p c t e", e=4)[:, c0 : c0 + step],
+                    scaled[:].rearrange("p t (c e) -> p c t e", e=4)[:, c0 : c0 + step],
+                )
+            return grouped
+
+        def quantize_x(grouped, b, u):
+            nc.vector.quantize_mx(
+                out=x_codes[b][:, half(u)].bitcast(FP8X4),
+                scales=x_planes[b][:, half(u)],
+                in_=grouped[:].rearrange("p c t -> p (c t)"),
+            )
+
+        def first_pass_x(u, tag):
+            scaled = tile([P, 4, HALF], BF16, "xs0%d" % u, tag)
+            for t in range(4):
+                scale_rows(scaled, picked[0][:, t, half(u)], t)
+            return interleave(scaled, 0, u, "grp%d" % u, 4)
+
+        one_slice(2)
+        later_loads(5)
+        one_slice(3)
+        later_loads(6)
+        one_slice(4)
+        later_loads(7)
+        wgo_t = tile([P, S], F32, "wgo", "wgs0")
+        nc.sync.dma_start(wgo_t[:], wgo)
+        result = []
+        for n, tag in enumerate(("bt00", "bt01", "tab_planes")):
+            dst = tile([P, T2], F32, "result%d" % n, tag)
+            nc.sync.dma_start(dst[:], page1[n * P : (n + 1) * P, :])
+            result.append(dst)
+        one_slice(5)
+        one_slice(6)
+        grouped0 = [first_pass_x(0, "base2")]
+        one_slice(7)
+        grouped0.append(first_pass_x(1, "base0"))
+        x_codes[0] = tile([P, S], U32, "xc0", "th1")
+        x_planes[0] = tile([P, S], U8, "xp0")
+        for u in range(2):
+            quantize_x(grouped0[u], 0, u)
+        x_codes[1] = tile([P, S], U32, "xc1", "codes1")
+        x_planes[1] = tile([P, S], U8, "xp1")
+
+        e = {}
+
+        def e_pass(u, n, step):
+            cols = slice(n * P, (n + 1) * P)
+            codes, planes = (v_words[step], v_planes[step]) if step < 2 else (x_codes[step - 2], x_planes[step - 2])
+            nc.tensor.matmul_mx(
+                out=e[u, n][:],
+                lhsT=w34_codes[:, step, cols].bitcast(FP8X4),
+                lhsT_scale=w34_planes[:, step, cols],
+                rhs=codes[:, half(u)].bitcast(FP8X4),
+                rhs_scale=planes[:, half(u)],
+                start=(step == 0),
+                stop=(step == 3),
+            )
+
+        def open_e(u, n, tag):
+            e[u, n] = bank("e%d%d" % (u, n), tag)
+            for step in range(3):
+                e_pass(u, n, step)
+
+        for (u, n), tag in (((0, 0), "state1"), ((0, 1), "state0"), ((0, 2), "t11"), ((1, 0), "t10")):
+            open_e(u, n, tag)
+
+        late45 = tile([P, 2, HALF], F32, "late45", "wgs23")
+        for t in range(2):
+            nc.vector.tensor_copy(late45[:, t, :], page[4 + t][:].indirect(list_half(idx3, 1)))
+        scaled_a = tile([P, 4, HALF], BF16, "xs10", "bt11")
+        for t in range(4):
+            scale_rows(scaled_a, picked[1][:, t, :], 4 + t)
+        quantize_x(interleave(scaled_a, 1, 0, "grp0"), 1, 0)
+        late67 = tile([P, 2, HALF], F32, "late67", "grp0")
+        for t in range(2):
+            nc.vector.tensor_copy(late67[:, t, :], page[6 + t][:].indirect(list_half(idx3, 1)))
+
+        y = [tile([P, S], F32, "y%d" % n, "h%d" % ((n + 2) % 3)) for n in range(3)]
+
+        def features(u, n):
+            e_pass(u, n, 3)
+            sq = tile([P, HALF], F32, "sq%d%d" % (u, n), "bt11")
+            nc.scalar.activation(sq[:], e[u, n][:], ACT.Square)
+            nc.scalar.activation(y[n][:, half(u)], sq[:], ACT.Ln, bias=1.0)
+            nc.vector.tensor_tensor(
+                result[n][:].indirect(list_half(idx4, u)), y[n][:, half(u)], wgo_t[:, half(u)], MULT
+            )
+
+        features(0, 0)
+        features(0, 1)
+        open_e(1, 1, "state1")
+        open_e(1, 2, "state0")
+        scaled_b = tile([P, 4, HALF], BF16, "xs11", "bt11")
+        for t in range(4):
+            scale_rows(scaled_b, (late45, late67)[t // 2][:, t % 2, :], 4 + t)
+        quantize_x(interleave(scaled_b, 1, 1, "grp1"), 1, 1)
+        features(0, 2)
+        for n in range(3):
+            features(1, n)
+            nc.sync.dma_start(out[n * P : (n + 1) * P, :], result[n][:])

@@ -68,12 +68,12 @@ def tile_list_radon_mitigation_page_kernel(
             )
             return words
 
-        def load_wgs(t0, t1, name, pieces):
-            dst = tile([P, t1 - t0, S], F32, name)
-            rows = wgs.rearrange("(q t) j -> q t j", t=4)[:, t0:t1, :]
+        def load_wgs(t, pieces):
+            dst = tile([P, S], F32, "wgs%d" % t)
+            rows = wgs.rearrange("(q t) j -> q t j", t=4)[:, t, :]
             for cols in pieces:
                 for quad in QUADS:
-                    nc.sync.dma_start(dst[32 * quad : 32 * quad + 32, :, cols], rows[:, :, cols])
+                    nc.sync.dma_start(dst[32 * quad : 32 * quad + 32, cols], rows[:, cols])
             return dst
 
         tab_planes = tile([P, 2, T], U8, "tab_planes")
@@ -108,20 +108,11 @@ def tile_list_radon_mitigation_page_kernel(
         w1_raw[0, 1] = load_weight(w1, 1, half(0), "w1raw01", "raw1")
         base_t = {0: load_rows(base, 0, 0, "base0", "base0")}
         page = {0: load_rows(page0, 0, 0, "page0", "page0")}
-        wgs0 = load_wgs(0, 1, "wgs0", (half(0), half(1)))
+        wgs_t = [load_wgs(0, (half(0), half(1)))]
         base_t[1] = load_rows(base, 0, 1, "base1", "base1")
         page[1] = load_rows(page0, 0, 1, "page1", "page1")
-        wgs1 = load_wgs(1, 2, "wgs1", (slice(0, S),))
+        wgs_t.append(load_wgs(1, (slice(0, S),)))
         base_t[2] = load_rows(base, 0, 2, "base2", "base2")
-        page[2] = load_rows(page0, 0, 2, "page2", "page2")
-        wgs23 = load_wgs(2, 4, "wgs23", (slice(0, S),))
-        for a in range(2):
-            w1_raw[1, a] = load_weight(w1, a, half(1), "w1raw1%d" % a, "raw%d" % (2 + a))
-        w2w[1] = load_w2(1)
-        page[3] = load_rows(page0, 0, 3, "page3", "page3")
-        gains = tile([P, 2, 4], F32, "gains")
-        nc.sync.dma_start(gains[:], gain.rearrange("(b p t) -> p b t", b=2, t=4))
-        idx4 = load_list(offs4, "idx4")
 
         v_planes = [tile([P, S], U8, "v_plane%d" % a) for a in range(2)]
         for a in range(2):
@@ -149,9 +140,11 @@ def tile_list_radon_mitigation_page_kernel(
                     )
                     done += width
 
-        for b in range(2):
+        def open_w1(b):
             w1_codes[b] = tile([P, 2, HALF], U32, "w1c%d" % b, "codes%d" % b)
             w1_planes[b] = tile([P, 2, HALF], U8, "w1s%d" % b)
+
+        open_w1(0)
         v_words = [tile([P, S], U32, "v%d" % a) for a in range(2)]
         nc.vector.tensor_copy(v_words[0][:], tab[0][:].bitcast(U32).indirect(idx[:]))
         for u in range(2):
@@ -165,7 +158,7 @@ def tile_list_radon_mitigation_page_kernel(
             b_t[b, u] = tile([P, 4, 4, P], F32, "bt%d%d" % (b, u))
             for jb in range(4):
                 cols = slice(u * HALF + jb * P, u * HALF + (jb + 1) * P)
-                acc = bank("pb%d%d%d" % (b, u, jb), "pb%d" % jb)
+                acc = bank("pb%d%d%d" % (b, u, jb), "pb%d" % (jb % 2) if b else ("pb0", "pb1", "t10", "t11")[jb])
                 for a in range(2):
                     nc.tensor.matmul_mx(
                         out=acc[:],
@@ -192,7 +185,7 @@ def tile_list_radon_mitigation_page_kernel(
         def first_product(s, u):
             b, t = divmod(s, 4)
             rows = slice(t * P, (t + 1) * P)
-            acc = bank("pa%d%d" % (s, u), "state%d" % u)
+            acc = bank("pa%d%d" % (s, u), "swap%d%d" % (b, u))
             for a in range(2):
                 nc.tensor.matmul_mx(
                     out=acc[:],
@@ -216,48 +209,49 @@ def tile_list_radon_mitigation_page_kernel(
             quantize_w1(0, 1, 1, 4, nc.vector.tensor_copy, "grp1")
             for u in range(2):
                 skip_product(0, u)
-                post = bank("post_first%d" % u, "t1%d" % u)
+                post = bank("post_first%d" % u, "swap1%d" % u)
                 add_transposed(post, lambda jb: b_t[0, u][:, jb, 0, :])
                 nc.vector.tensor_tensor(h[0][:, half(u)], post[:], th[u][:], ADD)
                 nc.vector.tensor_tensor(
-                    page[0][:].indirect(list_half(idx2, u)), h[0][:, half(u)], wgs0[:, 0, half(u)], MULT
+                    page[0][:].indirect(list_half(idx2, u)), h[0][:, half(u)], wgs_t[0][:, half(u)], MULT
                 )
 
-        def state_half(s, u):
-            b, t = divmod(s, 4)
-            acc = first_product(s, u)
-            a_sb = tile([P, HALF], F32, "a%d%d" % (s, u), "asb%d" % u)
-            nc.scalar.copy(a_sb[:], acc[:])
-            pre = bank("pre%d%d" % (s, u), "t1%d" % u)
-            add_transposed(
-                pre,
-                lambda jb: base_t[s][:, u * HALF + jb * P : u * HALF + (jb + 1) * P],
-                lambda jb: a_sb[:, jb * P : (jb + 1) * P],
-            )
-            th = tile([P, HALF], F32, "th%d%d" % (s, u), "th%d" % u)
-            nc.scalar.activation(th[:], pre[:], ACT.Tanh)
-            tanh_t[s, u] = th
-            if s == 4:
-                skip_product(b, u)
-            post = bank("post%d%d" % (s, u), "state%d" % u)
-            add_transposed(post, lambda jb: th[:, jb * P : (jb + 1) * P], lambda jb: b_t[b, u][:, jb, t, :])
-            nc.scalar.copy(h[s][:, half(u)], post[:])
+        def blocks_of(src, first=0):
+            return lambda jb: src[:, first + jb * P : first + (jb + 1) * P]
 
-        def wgs_of(s):
-            t = s % 4
-            return (wgs0[:, 0, :], wgs1[:, 0, :], wgs23[:, 0, :], wgs23[:, 1, :])[t]
+        def state(s):
+            b, t = divmod(s, 4)
+            a_sb, pre, post = [], [], []
+            for u in range(2):
+                acc = first_product(s, u)
+                a_sb.append(tile([P, HALF], F32, "a%d%d" % (s, u), "asb%d" % u))
+                nc.scalar.copy(a_sb[u][:], acc[:])
+            for u in range(2):
+                pre.append(bank("pre%d%d" % (s, u), "t1%d" % u))
+                add_transposed(pre[u], blocks_of(base_t[s], u * HALF), blocks_of(a_sb[u]))
+            for u in range(2):
+                tanh_t[s, u] = tile([P, HALF], F32, "th%d%d" % (s, u), "th%d" % u)
+                nc.scalar.activation(tanh_t[s, u][:], pre[u][:], ACT.Tanh)
+            for u in range(2):
+                post.append(bank("post%d%d" % (s, u), "swap%d%d" % (1 - b, u)))
+                add_transposed(post[u], blocks_of(tanh_t[s, u]), lambda jb: b_t[b, u][:, jb, t, :])
+            for u in range(2):
+                nc.scalar.copy(h[s][:, half(u)], post[u][:])
 
         picked = {}
 
         def one_slice(s):
             b, t = divmod(s, 4)
-            h[s] = tile([P, S], F32, "h%d" % s, "h%d" % (s % 3))
+            if s == 6:
+                last_h = tile([P, 2, S], F32, "h67", "tab_planes")
+                h[6], h[7] = last_h[:, 0, :], last_h[:, 1, :]
+            elif s < 6:
+                h[s] = tile([P, S], F32, "h%d" % s, "h%d" % (s % 3))
             if s == 0:
                 first_state()
             else:
-                for u in range(2):
-                    state_half(s, u)
-                nc.vector.tensor_tensor(page[s][:].indirect(idx2[:]), h[s][:], wgs_of(s), MULT)
+                state(s)
+                nc.vector.tensor_tensor(page[s][:].indirect(idx2[:]), h[s][:], wgs_t[t][:], MULT)
             if b == 0:
                 nc.vector.tensor_copy(picked[0][:, t, :], page[s][:].indirect(idx3[:]))
             else:
@@ -272,23 +266,35 @@ def tile_list_radon_mitigation_page_kernel(
         picked[0] = tile([P, 4, S], F32, "picked0", "big0")
         picked[1] = tile([P, 4, HALF], F32, "picked1", "big1")
         one_slice(0)
+        for a in range(2):
+            w1_raw[1, a] = load_weight(w1, a, half(1), "w1raw1%d" % a, "raw%d" % (2 + a))
         later_loads(3)
+        page[2] = load_rows(page0, 0, 2, "page2", "page2")
+        wgs_t.append(load_wgs(2, (slice(0, S),)))
+        w2w[1] = load_w2(1)
         one_slice(1)
+        open_w1(1)
         for a in range(2):
             quantize_w1(1, a, 0, 4, nc.scalar.copy, "grp%d" % a, 4)
-        later_loads(4)
+        base_t[4] = load_rows(base, 1, 0, "base4", "base1")
+        wgs_t.append(load_wgs(3, (slice(0, S),)))
+        page[3] = load_rows(page0, 0, 3, "page3", "page3")
+        gains = tile([P, 2, 4], F32, "gains")
+        nc.sync.dma_start(gains[:], gain.rearrange("(b p t) -> p b t", b=2, t=4))
+        idx4 = load_list(offs4, "idx4")
+        page[4] = load_rows(page0, 1, 0, "page4", "page0")
 
-        w34_codes = tile([P, 4, N], U32, "w34c")
-        w34_planes = tile([P, 4, N], U8, "w34s")
-        for m, src in enumerate((w4, w3)):
-            grouped = tile([P, 2, N, 4], BF16, "w34g%d" % m, "raw%d" % (2 + m))
+        def group_w34(m):
+            grouped = tile([P, 2, N, 4], BF16, "w34g%d" % m, "bt0%d" % m)
             for a in range(2):
-                raw = load_weight(src, a, slice(0, N), "w34raw%d%d" % (m, a), "raw%d" % a)
                 for c0 in range(0, N // 4, 32):
                     nc.scalar.copy(
                         grouped[:, a].rearrange("p (c e) i -> p c i e", e=4)[:, c0 : c0 + 32],
-                        raw[:].rearrange("p i (c e) -> p c i e", e=4)[:, c0 : c0 + 32],
+                        w34_raw[2 * m + a][:].rearrange("p i (c e) -> p c i e", e=4)[:, c0 : c0 + 32],
                     )
+            return grouped
+
+        def quantize_w34(grouped, m):
             flat_in = grouped[:].rearrange("p a c i -> p (a c i)")
             flat_codes = w34_codes[:, 2 * m : 2 * m + 2, :].rearrange("p a c -> p (a c)")
             flat_planes = w34_planes[:, 2 * m : 2 * m + 2, :].rearrange("p a c -> p (a c)")
@@ -303,16 +309,15 @@ def tile_list_radon_mitigation_page_kernel(
 
         def scale_rows(dst, src, s):
             b, t = divmod(s, 4)
-            nc.scalar.activation(dst[:, t, :], src, ACT.Copy, scale=gains[:, b, t : t + 1])
+            nc.scalar.activation(dst[:, t // 2, :, t % 2], src, ACT.Copy, scale=gains[:, b, t : t + 1])
 
         def interleave(scaled, b, u, tag, pieces=1):
             grouped = tile([P, HALF, 4], BF16, "xg%d%d" % (b, u), tag)
-            step = HALF // 4 // pieces
-            for c0 in range(0, HALF // 4, step):
-                nc.scalar.copy(
-                    grouped[:].rearrange("p (c e) t -> p c t e", e=4)[:, c0 : c0 + step],
-                    scaled[:].rearrange("p t (c e) -> p c t e", e=4)[:, c0 : c0 + step],
-                )
+            step = HALF // pieces
+            words_out = grouped[:].rearrange("p c t -> p (c t)").bitcast(F32).rearrange("p (c w) -> p c w", w=2)
+            words_in = scaled[:].rearrange("p w c e -> p w (c e)").bitcast(F32).rearrange("p w c -> p c w")
+            for c0 in range(0, HALF, step):
+                nc.scalar.copy(words_out[:, c0 : c0 + step], words_in[:, c0 : c0 + step])
             return grouped
 
         def quantize_x(grouped, b, u):
@@ -323,29 +328,41 @@ def tile_list_radon_mitigation_page_kernel(
             )
 
         def first_pass_x(u, tag):
-            scaled = tile([P, 4, HALF], BF16, "xs0%d" % u, tag)
+            scaled = tile([P, 2, HALF, 2], BF16, "xs0%d" % u, tag)
             for t in range(4):
                 scale_rows(scaled, picked[0][:, t, half(u)], t)
-            return interleave(scaled, 0, u, "grp%d" % u, 4)
+            return interleave(scaled, 0, u, "grp%d" % u, 2)
 
         one_slice(2)
         later_loads(5)
         one_slice(3)
+        for u in range(2):
+            skip_product(1, u)
         later_loads(6)
         one_slice(4)
         later_loads(7)
+        w34_raw = [
+            load_weight(src, a, slice(0, N), "w34raw%d%d" % (m, a), "raw%d" % (2 * m + a))
+            for m, src in enumerate((w4, w3))
+            for a in range(2)
+        ]
         wgo_t = tile([P, S], F32, "wgo", "wgs0")
         nc.sync.dma_start(wgo_t[:], wgo)
-        result = []
-        for n, tag in enumerate(("bt00", "bt01", "tab_planes")):
-            dst = tile([P, T2], F32, "result%d" % n, tag)
-            nc.sync.dma_start(dst[:], page1[n * P : (n + 1) * P, :])
-            result.append(dst)
         one_slice(5)
+        w34_grouped = [group_w34(m) for m in range(2)]
+        w34_codes = tile([P, 4, N], U32, "w34c", "wgs1")
+        w34_planes = tile([P, 4, N], U8, "w34s")
+        for m in range(2):
+            quantize_w34(w34_grouped[m], m)
+        result = {}
+        for n, tag in enumerate(("bt00", "bt01", "raw0")):
+            result[n] = tile([P, T2], F32, "result%d" % n, tag)
+            nc.sync.dma_start(result[n][:], page1[n * P : (n + 1) * P, :])
         one_slice(6)
-        grouped0 = [first_pass_x(0, "base2")]
         one_slice(7)
-        grouped0.append(first_pass_x(1, "base0"))
+        warm = tile([P, 1], F32, "warm")
+        nc.scalar.activation(warm[:], tanh_t[7, 1][:, 0:1], ACT.Ln, bias=1.0, scale=0.0)
+        grouped0 = [first_pass_x(u, "base1") for u in range(2)]
         x_codes[0] = tile([P, S], U32, "xc0", "th1")
         x_planes[0] = tile([P, S], U8, "xp0")
         for u in range(2):
@@ -373,13 +390,13 @@ def tile_list_radon_mitigation_page_kernel(
             for step in range(3):
                 e_pass(u, n, step)
 
-        for (u, n), tag in (((0, 0), "state1"), ((0, 1), "state0"), ((0, 2), "t11"), ((1, 0), "t10")):
+        for (u, n), tag in (((0, 0), "swap01"), ((0, 1), "swap00"), ((0, 2), "t11"), ((1, 0), "t10")):
             open_e(u, n, tag)
 
-        late45 = tile([P, 2, HALF], F32, "late45", "wgs23")
+        late45 = tile([P, 2, HALF], F32, "late45", "wgs3")
         for t in range(2):
             nc.vector.tensor_copy(late45[:, t, :], page[4 + t][:].indirect(list_half(idx3, 1)))
-        scaled_a = tile([P, 4, HALF], BF16, "xs10", "bt11")
+        scaled_a = tile([P, 2, HALF, 2], BF16, "xs10", "base1")
         for t in range(4):
             scale_rows(scaled_a, picked[1][:, t, :], 4 + t)
         quantize_x(interleave(scaled_a, 1, 0, "grp0"), 1, 0)
@@ -387,11 +404,11 @@ def tile_list_radon_mitigation_page_kernel(
         for t in range(2):
             nc.vector.tensor_copy(late67[:, t, :], page[6 + t][:].indirect(list_half(idx3, 1)))
 
-        y = [tile([P, S], F32, "y%d" % n, "h%d" % ((n + 2) % 3)) for n in range(3)]
+        y = [tile([P, S], F32, "y%d" % n, "h%d" % n) for n in range(3)]
 
         def features(u, n):
             e_pass(u, n, 3)
-            sq = tile([P, HALF], F32, "sq%d%d" % (u, n), "bt11")
+            sq = tile([P, HALF], F32, "sq%d%d" % (u, n), "base1")
             nc.scalar.activation(sq[:], e[u, n][:], ACT.Square)
             nc.scalar.activation(y[n][:, half(u)], sq[:], ACT.Ln, bias=1.0)
             nc.vector.tensor_tensor(
@@ -400,9 +417,9 @@ def tile_list_radon_mitigation_page_kernel(
 
         features(0, 0)
         features(0, 1)
-        open_e(1, 1, "state1")
-        open_e(1, 2, "state0")
-        scaled_b = tile([P, 4, HALF], BF16, "xs11", "bt11")
+        open_e(1, 1, "swap01")
+        open_e(1, 2, "swap00")
+        scaled_b = tile([P, 2, HALF, 2], BF16, "xs11", "base1")
         for t in range(4):
             scale_rows(scaled_b, (late45, late67)[t // 2][:, t % 2, :], 4 + t)
         quantize_x(interleave(scaled_b, 1, 1, "grp1"), 1, 1)

@@ -349,6 +349,8 @@ def tile_list_radon_mitigation_page_kernel(
         wgo_t = tile([P, S], F32, "wgo", "wgs0")
         nc.sync.dma_start(wgo_t[:], wgo)
         one_slice(5)
+        one_slice(6)
+        one_slice(7)
         w34_grouped = [group_w34(m) for m in range(2)]
         w34_codes = tile([P, 4, N], U32, "w34c", "wgs1")
         w34_planes = tile([P, 4, N], U8, "w34s")
@@ -358,11 +360,9 @@ def tile_list_radon_mitigation_page_kernel(
         for n, tag in enumerate(("bt00", "bt01", "raw0")):
             result[n] = tile([P, T2], F32, "result%d" % n, tag)
             nc.sync.dma_start(result[n][:], page1[n * P : (n + 1) * P, :])
-        one_slice(6)
-        one_slice(7)
         warm = tile([P, 1], F32, "warm")
         nc.scalar.activation(warm[:], tanh_t[7, 1][:, 0:1], ACT.Ln, bias=1.0, scale=0.0)
-        grouped0 = [first_pass_x(u, "base1") for u in range(2)]
+        grouped0 = [first_pass_x(0, "base0"), first_pass_x(1, "base1")]
         x_codes[0] = tile([P, S], U32, "xc0", "th1")
         x_planes[0] = tile([P, S], U8, "xp0")
         for u in range(2):
@@ -408,9 +408,9 @@ def tile_list_radon_mitigation_page_kernel(
 
         def features(u, n):
             e_pass(u, n, 3)
-            sq = tile([P, HALF], F32, "sq%d%d" % (u, n), "base1")
-            nc.scalar.activation(sq[:], e[u, n][:], ACT.Square)
-            nc.scalar.activation(y[n][:, half(u)], sq[:], ACT.Ln, bias=1.0)
+            sq = scaled_a[:, 1].rearrange("p c e -> p (c e)").bitcast(F32)
+            nc.scalar.activation(sq, e[u, n][:], ACT.Square)
+            nc.scalar.activation(y[n][:, half(u)], sq, ACT.Ln, bias=1.0)
             nc.vector.tensor_tensor(
                 result[n][:].indirect(list_half(idx4, u)), y[n][:, half(u)], wgo_t[:, half(u)], MULT
             )
@@ -419,7 +419,7 @@ def tile_list_radon_mitigation_page_kernel(
         features(0, 1)
         open_e(1, 1, "swap01")
         open_e(1, 2, "swap00")
-        scaled_b = tile([P, 2, HALF, 2], BF16, "xs11", "base1")
+        scaled_b = scaled_a
         for t in range(4):
             scale_rows(scaled_b, (late45, late67)[t // 2][:, t % 2, :], 4 + t)
         quantize_x(interleave(scaled_b, 1, 1, "grp1"), 1, 1)

from contextlib import ExitStack

import concourse.mybir as mybir
from concourse.masks import make_identity

K, T, S, H, N, T2 = 1024, 4096, 1024, 1024, 384, 2048
FLOPS = 2 * S * (2 * K * H + H * N + K * N)

F32 = mybir.dt.float32
BF16 = mybir.dt.bfloat16
I32 = mybir.dt.int32
U32 = mybir.dt.uint32
U16 = mybir.dt.uint16
U8 = mybir.dt.uint8
FP8X4 = mybir.dt.float8_e4m3fn_x4
FP4X4 = mybir.dt.float4_e2m1fn_x4
ACT = mybir.ActivationFunctionType
MULT = mybir.AluOpType.mult
ADD = mybir.AluOpType.add

P = 128
HALF = 512
LIST_HALF = HALF // 16
QUADS = (0, 2, 1, 3)


def tile_list_radon_mitigation_page_kernel(
    tc, tab_words, tab_scales, offs, w1, base, w2_words, w2_scales, wgs, page0, offs2, offs3,
    gain, w3, w4, wgo, page1, offs4, out,
):
    nc = tc.nc
    with ExitStack() as ctx:
        sb = ctx.enter_context(tc.tile_pool(name="sb", bufs=1))
        ps = ctx.enter_context(tc.psum_pool(name="ps", bufs=1))

        def tile(shape, dtype, name, tag=None):
            return sb.tile(shape, dtype, name=name, tag=tag or name, align_bytes=64)

        def bank(name, tag):
            return ps.tile([P, HALF], F32, name=name, tag=tag)

        def half(u):
            return slice(u * HALF, (u + 1) * HALF)

        def list_half(lst, u):
            return lst[:, u * LIST_HALF : (u + 1) * LIST_HALF]

        def load_list(src, name):
            lst = tile([P, S // 16], U16, name)
            nc.sync.dma_start(lst[:], src)
            return lst

        def load_rows(src, b, t, name, tag):
            dst = tile([P, src.shape[1]], F32, name, tag)
            nc.sync.dma_start(dst[:], src[half(b), :].rearrange("(p t) j -> p t j", t=4)[:, t, :])
            return dst

        def load_weight(src, a, cols, name, tag):
            raw = tile([P, 4, cols.stop - cols.start], F32, name, tag)
            nc.sync.dma_start(raw[:], src[half(a), cols].rearrange("(p i) c -> p i c", i=4))
            return raw

        def load_w2(b):
            words = tile([P, 2, 2 * HALF], U8, "w2w%d" % b)
            nc.sync.dma_start(
                words[:].bitcast(I32),
                w2_words[:, :, 2 * HALF * b : 2 * HALF * (b + 1)].rearrange("a p c -> p a c").bitcast(I32),
            )
            return words

        def load_wgs(t, pieces):
            dst = tile([P, S], F32, "wgs%d" % t)
            rows = wgs.rearrange("(q t) j -> q t j", t=4)[:, t, :]
            for cols in pieces:
                for quad in QUADS:
                    nc.sync.dma_start(dst[32 * quad : 32 * quad + 32, cols], rows[:, cols])
            return dst

        tab_planes = tile([P, 2, T], U8, "tab_planes")
        w2_planes = tile([P, 2, H], U8, "w2_planes")
        nc.vector.memset(tab_planes[:, 0, :].bitcast(I32), 0)
        nc.gpsimd.memset(tab_planes[:, 1, :].bitcast(I32), 0)
        nc.vector.memset(w2_planes[:].bitcast(I32), 0)
        ident = tile([P, P], F32, "ident")
        make_identity(nc, ident[:])

        idx = load_list(offs, "idx")
        tab = [tile([P, T], I32, "tab%d" % a, "big%d" % a) for a in range(2)]

        def load_tab(a):
            nc.sync.dma_start(tab[a][:], tab_words[a].rearrange("p t i -> p (t i)").bitcast(I32))

        def load_planes(planes, src):
            for quad in QUADS:
                nc.sync.dma_start(
                    planes[32 * quad : 32 * quad + 4].bitcast(I32),
                    src[:, 4 * quad : 4 * quad + 4, :].rearrange("a r c -> r a c").bitcast(I32),
                )

        load_tab(0)
        w2w = {0: load_w2(0)}
        idx2 = load_list(offs2, "idx2")
        idx3 = load_list(offs3, "idx3")
        load_planes(tab_planes, tab_scales)
        w1_raw = {(0, 0): load_weight(w1, 0, half(0), "w1raw00", "raw0")}
        load_tab(1)
        load_planes(w2_planes, w2_scales)
        w1_raw[0, 1] = load_weight(w1, 1, half(0), "w1raw01", "raw1")
        base_t = {0: load_rows(base, 0, 0, "base0", "base0")}
        page = {0: load_rows(page0, 0, 0, "page0", "page0")}
        wgs_t = [load_wgs(0, (half(0), half(1)))]
        base_t[1] = load_rows(base, 0, 1, "base1", "base1")
        page[1] = load_rows(page0, 0, 1, "page1", "page1")
        wgs_t.append(load_wgs(1, (slice(0, S),)))
        base_t[2] = load_rows(base, 0, 2, "base2", "base2")

        v_planes = [tile([P, S], U8, "v_plane%d" % a) for a in range(2)]
        for a in range(2):
            nc.vector.tensor_copy(v_planes[a][:], tab_planes[:, a, :].indirect(idx[:]))

        w1_codes, w1_planes = {}, {}

        def quantize_w1(b, a, t0, t1, copy, tag, pieces=1):
            grouped = tile([P, t1 - t0, P, 4], BF16, "w1g%d%d%d" % (b, a, t0), tag)
            step = P // pieces
            for m0 in range(0, P, step):
                copy(
                    grouped[:].rearrange("p t m i -> p m i t")[:, m0 : m0 + step],
                    w1_raw[b, a][:].rearrange("p i (m t) -> p m i t", t=4)[:, m0 : m0 + step, :, t0:t1],
                )
            flat = grouped[:].rearrange("p t m i -> p (t m i)")
            done = 0
            for width in (4, 2, 1):
                if (t1 - t0) & width:
                    cols = slice((t0 + done) * P, (t0 + done + width) * P)
                    nc.vector.quantize_mx(
                        out=w1_codes[b][:, a, cols].bitcast(FP8X4),
                        scales=w1_planes[b][:, a, cols],
                        in_=flat[:, done * HALF : (done + width) * HALF],
                    )
                    done += width

        def open_w1(b):
            w1_codes[b] = tile([P, 2, HALF], U32, "w1c%d" % b, "codes%d" % b)
            w1_planes[b] = tile([P, 2, HALF], U8, "w1s%d" % b)

        open_w1(0)
        v_words = [tile([P, S], U32, "v%d" % a) for a in range(2)]
        nc.vector.tensor_copy(v_words[0][:], tab[0][:].bitcast(U32).indirect(idx[:]))
        for u in range(2):
            nc.vector.tensor_copy(v_words[1][:, half(u)], tab[1][:].bitcast(U32).indirect(list_half(idx, u)))

        quantize_w1(0, 0, 0, 4, nc.scalar.copy, "grp0")
        quantize_w1(0, 1, 0, 1, nc.vector.tensor_copy, "grp1")
        b_t = {}

        def skip_product(b, u):
            b_t[b, u] = tile([P, 4, 4, P], F32, "bt%d%d" % (b, u))
            for jb in range(4):
                cols = slice(u * HALF + jb * P, u * HALF + (jb + 1) * P)
                acc = bank("pb%d%d%d" % (b, u, jb), "pb%d" % (jb % 2) if b else ("pb0", "pb1", "t10", "t11")[jb])
                for a in range(2):
                    nc.tensor.matmul_mx(
                        out=acc[:],
                        lhsT=v_words[a][:, cols].bitcast(FP8X4),
                        lhsT_scale=v_planes[a][:, cols],
                        rhs=w2w[b][:, a, :].bitcast(FP4X4),
                        rhs_scale=w2_planes[:, a, half(b)],
                        start=(a == 0),
                        stop=(a == 1),
                    )
                nc.scalar.copy(b_t[b, u][:, jb], acc[:].rearrange("p (q t) -> p t q", t=4))

        def add_transposed(acc, *terms):
            for n, blocks in enumerate(terms):
                for jb in range(4):
                    nc.tensor.matmul(
                        acc[:, jb * P : (jb + 1) * P], lhsT=blocks(jb), rhs=ident[:], is_transpose=True,
                        start=(n == 0 and jb == 0), stop=(n == len(terms) - 1 and jb == 3),
                    )

        h = {}
        tanh_t = {}

        def first_product(s, u):
            b, t = divmod(s, 4)
            rows = slice(t * P, (t + 1) * P)
            acc = bank("pa%d%d" % (s, u), "swap%d%d" % (b, u))
            for a in range(2):
                nc.tensor.matmul_mx(
                    out=acc[:],
                    lhsT=w1_codes[b][:, a, rows].bitcast(FP8X4),
                    lhsT_scale=w1_planes[b][:, a, rows],
                    rhs=v_words[a][:, half(u)].bitcast(FP8X4),
                    rhs_scale=v_planes[a][:, half(u)],
                    start=(a == 0),
                    stop=(a == 1),
                )
            return acc

        def first_state():
            th = []
            for u in range(2):
                acc = first_product(0, u)
                pre = tile([P, HALF], F32, "pre_first%d" % u, "asb%d" % u)
                nc.vector.tensor_tensor(pre[:], acc[:], base_t[0][:, half(u)], ADD)
                th.append(tile([P, HALF], F32, "th_first%d" % u, "th%d" % u))
                nc.scalar.activation(th[u][:], pre[:], ACT.Tanh)
            quantize_w1(0, 1, 1, 4, nc.vector.tensor_copy, "grp1")
            for u in range(2):
                skip_product(0, u)
                post = bank("post_first%d" % u, "swap1%d" % u)
                add_transposed(post, lambda jb: b_t[0, u][:, jb, 0, :])
                nc.vector.tensor_tensor(h[0][:, half(u)], post[:], th[u][:], ADD)
                nc.vector.tensor_tensor(
                    page[0][:].indirect(list_half(idx2, u)), h[0][:, half(u)], wgs_t[0][:, half(u)], MULT
                )

        def blocks_of(src, first=0):
            return lambda jb: src[:, first + jb * P : first + (jb + 1) * P]

        def state(s):
            b, t = divmod(s, 4)
            a_sb, pre, post = [], [], []
            for u in range(2):
                acc = first_product(s, u)
                a_sb.append(tile([P, HALF], F32, "a%d%d" % (s, u), "asb%d" % u))
                nc.scalar.copy(a_sb[u][:], acc[:])
            for u in range(2):
                pre.append(bank("pre%d%d" % (s, u), "t1%d" % u))
                add_transposed(pre[u], blocks_of(base_t[s], u * HALF), blocks_of(a_sb[u]))
            for u in range(2):
                tanh_t[s, u] = tile([P, HALF], F32, "th%d%d" % (s, u), "th%d" % u)
                nc.scalar.activation(tanh_t[s, u][:], pre[u][:], ACT.Tanh)
            for u in range(2):
                post.append(bank("post%d%d" % (s, u), "swap%d%d" % (1 - b, u)))
                add_transposed(post[u], blocks_of(tanh_t[s, u]), lambda jb: b_t[b, u][:, jb, t, :])
            for u in range(2):
                nc.scalar.copy(h[s][:, half(u)], post[u][:])

        picked = {}

        def one_slice(s):
            b, t = divmod(s, 4)
            if s == 6:
                last_h = tile([P, 2, S], F32, "h67", "tab_planes")
                h[6], h[7] = last_h[:, 0, :], last_h[:, 1, :]
            elif s < 6:
                h[s] = tile([P, S], F32, "h%d" % s, "h%d" % (s % 3))
            if s == 0:
                first_state()
            else:
                state(s)
                nc.vector.tensor_tensor(page[s][:].indirect(idx2[:]), h[s][:], wgs_t[t][:], MULT)
            if b == 0:
                nc.vector.tensor_copy(picked[0][:, t, :], page[s][:].indirect(idx3[:]))
            else:
                nc.vector.tensor_copy(picked[1][:, t, :], page[s][:].indirect(list_half(idx3, 0)))

        def later_loads(s):
            b, t = divmod(s, 4)
            base_t[s] = load_rows(base, b, t, "base%d" % s, "base%d" % (s % 3))
            if s >= 4:
                page[s] = load_rows(page0, b, t, "page%d" % s, "page%d" % (s % 4))

        picked[0] = tile([P, 4, S], F32, "picked0", "big0")
        picked[1] = tile([P, 4, HALF], F32, "picked1", "big1")
        one_slice(0)
        for a in range(2):
            w1_raw[1, a] = load_weight(w1, a, half(1), "w1raw1%d" % a, "raw%d" % (2 + a))
        later_loads(3)
        page[2] = load_rows(page0, 0, 2, "page2", "page2")
        wgs_t.append(load_wgs(2, (slice(0, S),)))
        w2w[1] = load_w2(1)
        one_slice(1)
        open_w1(1)
        for a in range(2):
            quantize_w1(1, a, 0, 4, nc.scalar.copy, "grp%d" % a, 4)
        base_t[4] = load_rows(base, 1, 0, "base4", "base1")
        wgs_t.append(load_wgs(3, (slice(0, S),)))
        page[3] = load_rows(page0, 0, 3, "page3", "page3")
        gains = tile([P, 2, 4], F32, "gains")
        nc.sync.dma_start(gains[:], gain.rearrange("(b p t) -> p b t", b=2, t=4))
        idx4 = load_list(offs4, "idx4")
        page[4] = load_rows(page0, 1, 0, "page4", "page0")

        def group_w34(m):
            grouped = tile([P, 2, N, 4], BF16, "w34g%d" % m, "bt0%d" % m)
            for a in range(2):
                for c0 in range(0, N // 4, 32):
                    nc.scalar.copy(
                        grouped[:, a].rearrange("p (c e) i -> p c i e", e=4)[:, c0 : c0 + 32],
                        w34_raw[2 * m + a][:].rearrange("p i (c e) -> p c i e", e=4)[:, c0 : c0 + 32],
                    )
            return grouped

        def quantize_w34(grouped, m):
            flat_in = grouped[:].rearrange("p a c i -> p (a c i)")
            flat_codes = w34_codes[:, 2 * m : 2 * m + 2, :].rearrange("p a c -> p (a c)")
            flat_planes = w34_planes[:, 2 * m : 2 * m + 2, :].rearrange("p a c -> p (a c)")
            for c0, c1 in ((0, 512), (512, 768)):
                nc.vector.quantize_mx(
                    out=flat_codes[:, c0:c1].bitcast(FP8X4),
                    scales=flat_planes[:, c0:c1],
                    in_=flat_in[:, 4 * c0 : 4 * c1],
                )

        x_codes, x_planes = {}, {}

        def scale_rows(dst, src, s):
            b, t = divmod(s, 4)
            nc.scalar.activation(dst[:, t // 2, :, t % 2], src, ACT.Copy, scale=gains[:, b, t : t + 1])

        def interleave(scaled, b, u, tag, pieces=1):
            grouped = tile([P, HALF, 4], BF16, "xg%d%d" % (b, u), tag)
            step = HALF // pieces
            words_out = grouped[:].rearrange("p c t -> p (c t)").bitcast(F32).rearrange("p (c w) -> p c w", w=2)
            words_in = scaled[:].rearrange("p w c e -> p w (c e)").bitcast(F32).rearrange("p w c -> p c w")
            for c0 in range(0, HALF, step):
                nc.scalar.copy(words_out[:, c0 : c0 + step], words_in[:, c0 : c0 + step])
            return grouped

        def quantize_x(grouped, b, u):
            nc.vector.quantize_mx(
                out=x_codes[b][:, half(u)].bitcast(FP8X4),
                scales=x_planes[b][:, half(u)],
                in_=grouped[:].rearrange("p c t -> p (c t)"),
            )

        def first_pass_x(u, tag):
            scaled = tile([P, 2, HALF, 2], BF16, "xs0%d" % u, tag)
            for t in range(4):
                scale_rows(scaled, picked[0][:, t, half(u)], t)
            return interleave(scaled, 0, u, "grp%d" % u, 2)

        one_slice(2)
        later_loads(5)
        one_slice(3)
        for u in range(2):
            skip_product(1, u)
        later_loads(6)
        one_slice(4)
        later_loads(7)
        w34_raw = [
            load_weight(src, a, slice(0, N), "w34raw%d%d" % (m, a), "raw%d" % (2 * m + a))
            for m, src in enumerate((w4, w3))
            for a in range(2)
        ]
        wgo_t = tile([P, S], F32, "wgo", "wgs0")
        nc.sync.dma_start(wgo_t[:], wgo)
        one_slice(5)
        one_slice(6)
        one_slice(7)
        w34_grouped = [group_w34(m) for m in range(2)]
        w34_codes = tile([P, 4, N], U32, "w34c", "wgs1")
        w34_planes = tile([P, 4, N], U8, "w34s")
        for m in range(2):
            quantize_w34(w34_grouped[m], m)
        result = {}
        for n, tag in enumerate(("bt00", "bt01", "raw0")):
            result[n] = tile([P, T2], F32, "result%d" % n, tag)
            nc.sync.dma_start(result[n][:], page1[n * P : (n + 1) * P, :])
        warm = tile([P, 1], F32, "warm")
        nc.scalar.activation(warm[:], tanh_t[7, 1][:, 0:1], ACT.Ln, bias=1.0, scale=0.0)
        grouped0 = [first_pass_x(0, "base0"), first_pass_x(1, "base1")]
        x_codes[0] = tile([P, S], U32, "xc0", "th1")
        x_planes[0] = tile([P, S], U8, "xp0")
        for u in range(2):
            quantize_x(grouped0[u], 0, u)
        x_codes[1] = tile([P, S], U32, "xc1", "codes1")
        x_planes[1] = tile([P, S], U8, "xp1")

        e = {}

        def e_pass(u, n, step):
            cols = slice(n * P, (n + 1) * P)
            codes, planes = (v_words[step], v_planes[step]) if step < 2 else (x_codes[step - 2], x_planes[step - 2])
            nc.tensor.matmul_mx(
                out=e[u, n][:],
                lhsT=w34_codes[:, step, cols].bitcast(FP8X4),
                lhsT_scale=w34_planes[:, step, cols],
                rhs=codes[:, half(u)].bitcast(FP8X4),
                rhs_scale=planes[:, half(u)],
                start=(step == 0),
                stop=(step == 3),
            )

        def open_e(u, n, tag):
            e[u, n] = bank("e%d%d" % (u, n), tag)
            for step in range(3):
                e_pass(u, n, step)

        for (u, n), tag in (((0, 0), "swap01"), ((0, 1), "swap00"), ((0, 2), "t11"), ((1, 0), "t10")):
            open_e(u, n, tag)

        late45 = tile([P, 2, HALF], F32, "late45", "wgs3")
        for t in range(2):
            nc.vector.tensor_copy(late45[:, t, :], page[4 + t][:].indirect(list_half(idx3, 1)))
        scaled_a = tile([P, 2, HALF, 2], BF16, "xs10", "base1")
        for t in range(4):
            scale_rows(scaled_a, picked[1][:, t, :], 4 + t)
        quantize_x(interleave(scaled_a, 1, 0, "grp0"), 1, 0)
        late67 = tile([P, 2, HALF], F32, "late67", "grp0")
        for t in range(2):
            nc.vector.tensor_copy(late67[:, t, :], page[6 + t][:].indirect(list_half(idx3, 1)))

        y = [tile([P, S], F32, "y%d" % n, "h%d" % n) for n in range(3)]

        def features(u, n):
            e_pass(u, n, 3)
            sq = scaled_a[:, 1].rearrange("p c e -> p (c e)").bitcast(F32)
            nc.scalar.activation(sq, e[u, n][:], ACT.Square)
            nc.scalar.activation(y[n][:, half(u)], sq, ACT.Ln, bias=1.0)
            nc.vector.tensor_tensor(
                result[n][:].indirect(list_half(idx4, u)), y[n][:, half(u)], wgo_t[:, half(u)], MULT
            )

        features(0, 0)
        features(0, 1)
        open_e(1, 1, "swap01")
        open_e(1, 2, "swap00")
        scaled_b = scaled_a
        for t in range(4):
            scale_rows(scaled_b, (late45, late67)[t // 2][:, t % 2, :], 4 + t)
        quantize_x(interleave(scaled_b, 1, 1, "grp1"), 1, 1)
        features(0, 2)
        for n in range(3):
            features(1, n)
            nc.sync.dma_start(out[n * P : (n + 1) * P, :], result[n][:])
